import numpy as np
import ml_dtypes


def mxq(x, axis, fmt="e4m3"):
    dtype, down = {"e4m3": (ml_dtypes.float8_e4m3fn, 7), "e5m2": (ml_dtypes.float8_e5m2, 14)}[fmt]
    v = np.moveaxis(np.asarray(x, np.float32).astype(ml_dtypes.bfloat16).astype(np.float64), axis, -1)
    blocks = v.reshape(v.shape[:-1] + (-1, 32))
    amax = np.abs(blocks).max(-1, keepdims=True)
    byte = np.maximum(np.where(amax > 0, np.frexp(amax)[1] - 1 + 127, 0) - down, 1)
    scale = np.exp2(byte - 127.0)
    codes = (blocks / scale).astype(np.float32).astype(dtype).astype(np.float64)
    return np.moveaxis((codes * scale).reshape(v.shape), -1, axis)


WIDE = False


def mx_kscale(k):
    if not WIDE:
        return np.ones(k)
    levels = np.array([18, -18])
    if k % 512:
        return np.exp2(np.random.permutation(np.resize(levels, k // 32))).repeat(32)
    a = np.empty((k // 512, 16))
    for p in range(k // 512):
        a[p, :8] = np.random.permutation(np.resize(levels, 8))
        for g in range(8):
            far = levels[np.abs(levels - a[p, g]) >= 10]
            a[p, g + 8] = far[np.random.randint(len(far))]
    return np.exp2(a.ravel()).repeat(32)


def f64(x):
    return np.asarray(x).astype(np.float64)


def striped(idx):
    return np.tile(np.asarray(idx).reshape(-1, 16).T, (8, 1)).astype(np.uint16)


def unstriped(offs):
    return offs[:16].T.reshape(-1).astype(np.int64)


E2M1 = np.array([0.0, 0.5, 1.0, 1.5, 2.0, 3.0, 4.0, 6.0, -0.0, -0.5, -1.0, -1.5, -2.0, -3.0, -4.0, -6.0])


def pack_weight(w, fmt):
    k, n = w.shape
    w = f64(np.asarray(w, np.float32).astype(ml_dtypes.bfloat16)).reshape(k // 32, 32, n)
    amax = np.abs(w).max(1)
    if fmt == "e4m3":
        byte = np.frexp(amax)[1] - 1 + 127 - 7
    else:
        mant, ex = np.frexp(amax / 6.0)
        byte = np.where(mant > 0.5, ex, ex - 1) + 127
    byte = np.clip(np.where(amax > 0, byte, 1), 1, 254)
    scaled = (w * np.exp2(127.0 - byte)[:, None, :]).reshape(k, n).astype(np.float32)
    by_word = np.ascontiguousarray(scaled.reshape(k // 512, 128, 4, n).transpose(0, 1, 3, 2))
    if fmt == "e4m3":
        words = by_word.astype(ml_dtypes.float8_e4m3fn).view(np.uint8)
    else:
        c = by_word.astype(ml_dtypes.float4_e2m1fn).view(np.uint8) & 0xF
        words = (c[..., 0::2] | (c[..., 1::2] << 4)).reshape(k // 512, 128, 2 * n)
    return np.ascontiguousarray(words), np.ascontiguousarray(byte.astype(np.uint8).reshape(k // 512, 16, n))


def unpack_weight(words, scales, fmt):
    g, _, n = scales.shape
    words = np.ascontiguousarray(words).reshape(g, 128, n, -1)
    if fmt == "e4m3":
        vals = words.view(ml_dtypes.float8_e4m3fn).astype(np.float64)
    else:
        nib = np.empty((g, 128, n, 4), np.uint8)
        nib[..., 0::2] = words & 0xF
        nib[..., 1::2] = words >> 4
        vals = E2M1[nib]
    vals = vals * np.repeat(np.exp2(scales.astype(np.float64) - 127.0), 8, axis=1)[..., None]
    return vals.transpose(0, 1, 3, 2).reshape(g * 512, n)


V, K, E, D, DV = 1024, 2, 2048, 256, 1024


def setup_inputs():
    n = np.random.standard_normal
    v = mx_kscale(DV)[:, None]
    coarse = lambda x: x.astype(np.float32).astype(ml_dtypes.bfloat16).astype(np.float64)
    wp = pack_weight(n((DV, D)) / np.sqrt(DV) / v, "e2m1")
    return {
        "dyT": (coarse(n((DV, V))) * v).astype(np.float32),
        "hE": (np.random.randint(-15, 16, (DV, E)) / 16.0).astype(np.float32),
        "ew": np.tile(np.random.randint(8, 33, E) / 16.0, (128, 1)).astype(np.float32),
        "w_words": wp[0],
        "w_scales": wp[1],
        "offs": striped(np.random.randint(0, V, E)),
        "offs2": striped(np.random.permutation(E)),
    }


def reference(dyT, hE, ew, w_words, w_scales, offs, offs2):
    h = f64(hE)
    dz = f64(ew)[:1] * f64(dyT)[:, unstriped(offs)] * (1.0 - h * h)
    dm = unpack_weight(w_words, w_scales, "e2m1").T @ mxq(dz, 0, "e5m2")
    return dm[:, unstriped(offs2)].reshape(D, V, K).sum(-1)

@@ -1,0 +1,118 @@
+from contextlib import ExitStack
+
+import concourse.mybir as mybir
+
+V, K, E, D, DV = 1024, 2, 2048, 256, 1024
+FLOPS = 2 * DV * D * E
+
+F32 = mybir.dt.float32
+BF16 = mybir.dt.bfloat16
+I32 = mybir.dt.int32
+U32 = mybir.dt.uint32
+U16 = mybir.dt.uint16
+U8 = mybir.dt.uint8
+E5M2X4 = mybir.dt.float8_e5m2_x4
+E2M1X4 = mybir.dt.float4_e2m1fn_x4
+MULT = mybir.AluOpType.mult
+ADD = mybir.AluOpType.add
+ACT = mybir.ActivationFunctionType
+
+P = 128
+PACK = 4
+PASSES = DV // (P * PACK)
+N = 512
+EDGES = 1024
+SPARE = 16
+
+
+def tile_attend_gmp_tnh_ew_kernel(tc, dyT, hE, ew, w_words, w_scales, offs, offs2, out):
+    nc = tc.nc
+    dy_planes = dyT.rearrange("(o p r) v -> o r p v", p=P, r=PACK)
+    h_planes = hE.rearrange("(o p r) e -> o r p e", p=P, r=PACK)
+    units = [(half, o) for half in range(E // EDGES) for o in range(PASSES)]
+
+    with ExitStack() as ctx:
+        keep = ctx.enter_context(tc.tile_pool(name="keep", bufs=1))
+        work = ctx.enter_context(tc.tile_pool(name="work", bufs=2))
+        psum = ctx.enter_context(tc.psum_pool(name="psum", bufs=1))
+
+        dst = keep.tile([P, E // 16], U16, name="dst")
+        src = keep.tile([P, E // 16], U16, name="src")
+        words = keep.tile([P, PASSES, 2 * D], U8, name="words", align_bytes=64)
+        w_sc = keep.tile([P, PASSES, D], U8, name="w_sc", align_bytes=64)
+        dy = {(o, r): keep.tile([P, V + SPARE], F32, name="dy%d%d" % (o, r)) for o in range(PASSES) for r in range(PACK)}
+        h = {(u, r): keep.tile([P, EDGES], F32, name="h%d%d" % (u, r)) for u in range(len(units)) for r in range(PACK)}
+        ew_sb = [keep.tile([P, EDGES], F32, name="ew%d" % half) for half in range(E // EDGES)]
+        dm = [keep.tile([P, E], F32, name="dm%d" % dh) for dh in range(D // P)]
+
+        for t in dy.values():
+            nc.gpsimd.memset(t[:, V:], 0.0)
+        nc.gpsimd.memset(w_sc[:].rearrange("p o d -> p (o d)").bitcast(U32), 0)
+        for q in range(4):
+            nc.gpsimd.dma_start(
+                out=w_sc[32 * q : 32 * q + 4, :, :].bitcast(I32),
+                in_=w_scales[:, 4 * q : 4 * q + 4, :].rearrange("o f d -> f o d").bitcast(I32),
+            )
+
+        nc.sync.dma_start(dst[:], offs)
+        for u, (half, o) in enumerate(units):
+            cols = slice(half * EDGES, (half + 1) * EDGES)
+            for r in range(PACK):
+                if half == 0:
+                    nc.sync.dma_start(out=dy[o, r][:, :V], in_=dy_planes[o, r])
+                if o == 0 and r == 0:
+                    nc.sync.dma_start(out=ew_sb[half][:], in_=ew[:, cols])
+                nc.sync.dma_start(out=h[u, r][:], in_=h_planes[o, r][:, cols])
+            if u == 0:
+                nc.sync.dma_start(out=words[:].bitcast(I32), in_=w_words.rearrange("o p b -> p o b").bitcast(I32))
+            if u == 1:
+                nc.sync.dma_start(src[:], offs2)
+
+        banks = {(c, dh): psum.tile([P, N], F32, name="bank%d%d" % (c, dh)) for c in range(E // N) for dh in range(D // P)}
+
+        for u, (half, o) in enumerate(units):
+            slope = work.tile([P, PACK, EDGES], F32, name="slope")
+            gew = work.tile([P, PACK, EDGES], F32, name="gew")
+            lst = dst[:, half * (EDGES // 16) : (half + 1) * (EDGES // 16)]
+            for r in range(PACK):
+                sq = work.tile([P, EDGES], F32, name="sq")
+                nc.scalar.activation(out=sq[:], in_=h[u, r][:], func=ACT.Square)
+                nc.scalar.activation(out=slope[:, r, :], in_=sq[:], func=ACT.Copy, scale=-1.0, bias=1.0)
+                nc.vector.tensor_tensor(gew[:, r, :], dy[o, r][:].indirect(lst), ew_sb[half][:], MULT)
+            dz = []
+            for j in range(EDGES // N):
+                z = work.tile([P, N, PACK], BF16, name="dz%d" % j, align_bytes=64)
+                cols = slice(j * N, (j + 1) * N)
+                nc.vector.tensor_tensor(
+                    z[:].rearrange("p (c i) t -> p c t i", i=2),
+                    gew[:, :, cols].rearrange("p t (c i) -> p c t i", i=2),
+                    slope[:, :, cols].rearrange("p t (c i) -> p c t i", i=2),
+                    MULT,
+                )
+                dz.append(z)
+            for j in range(EDGES // N):
+                c = half * (EDGES // N) + j
+                codes = work.tile([P, N], U32, name="codes%d" % j, align_bytes=64)
+                scales = work.tile([P, N], U8, name="scales%d" % j, align_bytes=64)
+                nc.vector.quantize_mx(out=codes[:].bitcast(E5M2X4), scales=scales[:], in_=dz[j][:].rearrange("p e t -> p (e t)"))
+                for dh in range(D // P):
+                    nc.tensor.matmul_mx(
+                        out=banks[c, dh][:],
+                        lhsT=words[:, o, 2 * P * dh : 2 * P * (dh + 1)].bitcast(E2M1X4),
+                        lhsT_scale=w_sc[:, o, P * dh : P * (dh + 1)],
+                        rhs=codes[:].bitcast(E5M2X4),
+                        rhs_scale=scales[:],
+                        start=(o == 0),
+                        stop=(o == PASSES - 1),
+                    )
+                    if o == PASSES - 1:
+                        nc.scalar.copy(out=dm[dh][:, c * N : (c + 1) * N], in_=banks[c, dh][:])
+
+        pieces = [(dh, a) for dh in range(D // P) for a in range(2)]
+        for dh, a in pieces:
+            picked = work.tile([P, EDGES], F32, name="picked")
+            nc.vector.tensor_copy(picked[:], dm[dh][:].indirect(src[:, a * (EDGES // 16) : (a + 1) * (EDGES // 16)]))
+            res = work.tile([P, EDGES // K], F32, name="res")
+            pairs = picked[:].rearrange("p (x j) -> p x j", j=K)
+            nc.vector.tensor_tensor(res[:], pairs[:, :, 0], pairs[:, :, 1], ADD)
+            nc.sync.dma_start(out=out[dh * P : (dh + 1) * P, a * (EDGES // K) : (a + 1) * (EDGES // K)], in_=res[:])

@@ -1,6 +1,7 @@
 from contextlib import ExitStack
 
 import concourse.mybir as mybir
+from concourse.masks import make_identity
 
 V, K, E, D, DV = 1024, 2, 2048, 256, 1024
 FLOPS = 2 * DV * D * E
@@ -21,15 +22,16 @@ P = 128
 PACK = 4
 PASSES = DV // (P * PACK)
 N = 512
-EDGES = 1024
+TURNED = 1024
+DIRECT = E - TURNED
 SPARE = 16
+CHUNKS = E // N
 
 
 def tile_attend_gmp_tnh_ew_kernel(tc, dyT, hE, ew, w_words, w_scales, offs, offs2, out):
     nc = tc.nc
     dy_planes = dyT.rearrange("(o p r) v -> o r p v", p=P, r=PACK)
     h_planes = hE.rearrange("(o p r) e -> o r p e", p=P, r=PACK)
-    units = [(half, o) for half in range(E // EDGES) for o in range(PASSES)]
 
     with ExitStack() as ctx:
         keep = ctx.enter_context(tc.tile_pool(name="keep", bufs=1))
@@ -41,78 +43,192 @@ def tile_attend_gmp_tnh_ew_kernel(tc, dyT, hE, ew, w_words, w_scales, offs, offs
         words = keep.tile([P, PASSES, 2 * D], U8, name="words", align_bytes=64)
         w_sc = keep.tile([P, PASSES, D], U8, name="w_sc", align_bytes=64)
         dy = {(o, r): keep.tile([P, V + SPARE], F32, name="dy%d%d" % (o, r)) for o in range(PASSES) for r in range(PACK)}
-        h = {(u, r): keep.tile([P, EDGES], F32, name="h%d%d" % (u, r)) for u in range(len(units)) for r in range(PACK)}
-        ew_sb = [keep.tile([P, EDGES], F32, name="ew%d" % half) for half in range(E // EDGES)]
+        first_t = keep.tile([P, PACK, TURNED], F32, name="first_t")
+        shared = keep.tile([P, PACK + 2, TURNED], F32, name="shared")
+        slope_t = [[first_t[:, r, :] for r in range(PACK)], [shared[:, 2 + (r + 2) % PACK, :] for r in range(PACK)]]
+        bank = [psum.tile([P, N], F32, name="bank%d" % i) for i in range(8)]
+        slope_d = [keep.tile([P, PACK, DIRECT], F32, name="slope_d%d" % o) for o in range(PASSES)]
+        ew_d = keep.tile([P, DIRECT], F32, name="ew_d")
+        ew_rows = keep.tile([P, P], F32, name="ew_rows")
+        ew_t = keep.tile([P, TURNED // P], F32, name="ew_t")
+        ident = keep.tile([P, P], F32, name="ident")
+        codes = [keep.tile([P, E], U32, name="codes%d" % o, align_bytes=64) for o in range(PASSES)]
+        scales = [keep.tile([P, E], U8, name="scales%d" % o, align_bytes=64) for o in range(PASSES)]
         dm = [keep.tile([P, E], F32, name="dm%d" % dh) for dh in range(D // P)]
 
         for t in dy.values():
-            nc.gpsimd.memset(t[:, V:], 0.0)
-        nc.gpsimd.memset(w_sc[:].rearrange("p o d -> p (o d)").bitcast(U32), 0)
+            nc.vector.memset(t[:, V:], 0.0)
+        nc.vector.memset(w_sc[:].rearrange("p o d -> p (o d)").bitcast(U32), 0)
+        nc.vector.memset(ew_rows[:], 0.0)
+        make_identity(nc, ident[:])
+
+        nc.sync.dma_start(dst[:], offs)
+        half = DIRECT // 2
+        for r in range(PACK):
+            nc.sync.dma_start(out=dy[0, r][:, :V], in_=dy_planes[0, r])
+            if r == 0:
+                nc.sync.dma_start(out=ew_d[:, :half], in_=ew[:, TURNED : TURNED + half])
+            nc.sync.dma_start(out=slope_t[0][r], in_=h_planes[0, r][:, :TURNED])
+            if r == 0:
+                nc.sync.dma_start(out=ew_d[:, half:], in_=ew[:, TURNED + half :])
+        for r in range(PACK):
+            nc.sync.dma_start(out=slope_d[0][:, r, :], in_=h_planes[0, r][:, TURNED:])
+        nc.sync.dma_start(out=ew_rows[: TURNED // P, :], in_=ew[0, :TURNED].rearrange("(b e) -> b e", e=P))
+        for r in range(PACK):
+            nc.sync.dma_start(out=dy[1, r][:, :V], in_=dy_planes[1, r])
+        for r in range(PACK):
+            nc.sync.dma_start(out=slope_t[1][r], in_=h_planes[1, r][:, :TURNED])
+        for r in range(PACK):
+            nc.sync.dma_start(out=slope_d[1][:, r, :], in_=h_planes[1, r][:, TURNED:])
+        nc.sync.dma_start(out=words[:].bitcast(I32), in_=w_words.rearrange("o p b -> p o b").bitcast(I32))
         for q in range(4):
-            nc.gpsimd.dma_start(
+            nc.sync.dma_start(
                 out=w_sc[32 * q : 32 * q + 4, :, :].bitcast(I32),
                 in_=w_scales[:, 4 * q : 4 * q + 4, :].rearrange("o f d -> f o d").bitcast(I32),
             )
+        nc.sync.dma_start(src[:], offs2)
 
-        nc.sync.dma_start(dst[:], offs)
-        for u, (half, o) in enumerate(units):
-            cols = slice(half * EDGES, (half + 1) * EDGES)
+        def listed(lst, a, b):
+            return lst[:, a // 16 : b // 16]
+
+        def make_slope(s):
+            for r in range(PACK + 1):
+                if r < PACK:
+                    nc.scalar.activation(out=s[r], in_=s[r], func=ACT.Square)
+                if r > 0:
+                    nc.scalar.activation(out=s[r - 1], in_=s[r - 1], func=ACT.Copy, scale=-1.0, bias=1.0)
+
+        def gather_direct(o, g, planes):
+            for r in planes:
+                cuts = [0, half, DIRECT] if (o, r) == (0, 0) else [0, DIRECT]
+                for a, b in zip(cuts, cuts[1:]):
+                    nc.vector.tensor_tensor(g[:, r, a:b], dy[o, r][:].indirect(listed(dst, TURNED + a, TURNED + b)), ew_d[:, a:b], MULT)
+
+        def gather_turned(o):
+            g = keep.tile([P, PACK, TURNED], F32, name="g_turned")
             for r in range(PACK):
-                if half == 0:
-                    nc.sync.dma_start(out=dy[o, r][:, :V], in_=dy_planes[o, r])
-                if o == 0 and r == 0:
-                    nc.sync.dma_start(out=ew_sb[half][:], in_=ew[:, cols])
-                nc.sync.dma_start(out=h[u, r][:], in_=h_planes[o, r][:, cols])
-            if u == 0:
-                nc.sync.dma_start(out=words[:].bitcast(I32), in_=w_words.rearrange("o p b -> p o b").bitcast(I32))
-            if u == 1:
-                nc.sync.dma_start(src[:], offs2)
+                nc.vector.tensor_tensor(g[:, r, :], dy[o, r][:].indirect(listed(dst, 0, TURNED)), slope_t[o][r], MULT)
+            return g
 
-        banks = {(c, dh): psum.tile([P, N], F32, name="bank%d%d" % (c, dh)) for c in range(E // N) for dh in range(D // P)}
+        def quantise(o, a, b, z):
+            nc.vector.quantize_mx(out=codes[o][:, a:b].bitcast(E5M2X4), scales=scales[o][:, a:b], in_=z)
 
-        for u, (half, o) in enumerate(units):
-            slope = work.tile([P, PACK, EDGES], F32, name="slope")
-            gew = work.tile([P, PACK, EDGES], F32, name="gew")
-            lst = dst[:, half * (EDGES // 16) : (half + 1) * (EDGES // 16)]
-            for r in range(PACK):
-                sq = work.tile([P, EDGES], F32, name="sq")
-                nc.scalar.activation(out=sq[:], in_=h[u, r][:], func=ACT.Square)
-                nc.scalar.activation(out=slope[:, r, :], in_=sq[:], func=ACT.Copy, scale=-1.0, bias=1.0)
-                nc.vector.tensor_tensor(gew[:, r, :], dy[o, r][:].indirect(lst), ew_sb[half][:], MULT)
-            dz = []
-            for j in range(EDGES // N):
-                z = work.tile([P, N, PACK], BF16, name="dz%d" % j, align_bytes=64)
+        def finish_direct(o, g):
+            made = []
+            for j in range(DIRECT // N):
+                z = work.tile([P, N * PACK], BF16, name="dz_direct", align_bytes=64)
                 cols = slice(j * N, (j + 1) * N)
                 nc.vector.tensor_tensor(
-                    z[:].rearrange("p (c i) t -> p c t i", i=2),
-                    gew[:, :, cols].rearrange("p t (c i) -> p c t i", i=2),
-                    slope[:, :, cols].rearrange("p t (c i) -> p c t i", i=2),
+                    z[:].rearrange("p (c i t) -> p c t i", i=2, t=PACK),
+                    g[:, :PACK, cols].rearrange("p t (c i) -> p c t i", i=2),
+                    slope_d[o][:, :, cols].rearrange("p t (c i) -> p c t i", i=2),
                     MULT,
                 )
-                dz.append(z)
-            for j in range(EDGES // N):
-                c = half * (EDGES // N) + j
-                codes = work.tile([P, N], U32, name="codes%d" % j, align_bytes=64)
-                scales = work.tile([P, N], U8, name="scales%d" % j, align_bytes=64)
-                nc.vector.quantize_mx(out=codes[:].bitcast(E5M2X4), scales=scales[:], in_=dz[j][:].rearrange("p e t -> p (e t)"))
-                for dh in range(D // P):
-                    nc.tensor.matmul_mx(
-                        out=banks[c, dh][:],
-                        lhsT=words[:, o, 2 * P * dh : 2 * P * (dh + 1)].bitcast(E2M1X4),
-                        lhsT_scale=w_sc[:, o, P * dh : P * (dh + 1)],
-                        rhs=codes[:].bitcast(E5M2X4),
-                        rhs_scale=scales[:],
-                        start=(o == 0),
-                        stop=(o == PASSES - 1),
-                    )
-                    if o == PASSES - 1:
-                        nc.scalar.copy(out=dm[dh][:, c * N : (c + 1) * N], in_=banks[c, dh][:])
+                made.append(z)
+            for j, z in enumerate(made):
+                quantise(o, TURNED + j * N, TURNED + (j + 1) * N, z[:])
 
-        pieces = [(dh, a) for dh in range(D // P) for a in range(2)]
-        for dh, a in pieces:
-            picked = work.tile([P, EDGES], F32, name="picked")
-            nc.vector.tensor_copy(picked[:], dm[dh][:].indirect(src[:, a * (EDGES // 16) : (a + 1) * (EDGES // 16)]))
-            res = work.tile([P, EDGES // K], F32, name="res")
-            pairs = picked[:].rearrange("p (x j) -> p x j", j=K)
-            nc.vector.tensor_tensor(res[:], pairs[:, :, 0], pairs[:, :, 1], ADD)
-            nc.sync.dma_start(out=out[dh * P : (dh + 1) * P, a * (EDGES // K) : (a + 1) * (EDGES // K)], in_=res[:])
+        def finish_turned(o, g):
+            blocks = TURNED // P
+            rows = {}
+            z = keep.tile([P, TURNED * PACK], BF16, name="dz_turned", align_bytes=64)
+            there = [bank[b % 4][:].rearrange("e (t p) -> e t p", t=PACK) for b in range(blocks)]
+            back = [bank[4 + pair % 2][:].rearrange("p (b u e) -> p b u e", b=2, u=2) for pair in range(blocks // 2)]
+
+            def turn(b):
+                for t in range(PACK):
+                    nc.tensor.transpose(there[b][:, t, :], g[:, t, b * P : (b + 1) * P], ident[:])
+
+            def weigh(b):
+                zt = work.tile([P, PACK * P], BF16, name="dz_rows", bufs=4)
+                nc.scalar.activation(
+                    out=zt[:].rearrange("e (u p w) -> e u p w", u=2, w=2),
+                    in_=there[b].rearrange("e (u w) p -> e u p w", w=2),
+                    func=ACT.Copy,
+                    scale=ew_t[:, b : b + 1],
+                )
+                rows[b] = zt
+
+            def turn_back(b):
+                for u in range(2):
+                    nc.tensor.transpose(back[b // 2][:, b % 2, u, :], rows[b][:].bitcast(F32)[:, u * P : (u + 1) * P], ident[:])
+
+            def lay(pair):
+                at = pair * N
+                nc.scalar.copy(
+                    out=z[:].bitcast(F32)[:, at : at + N].rearrange("p (b e u) -> p b e u", b=2, u=2),
+                    in_=back[pair].rearrange("p b u e -> p b e u"),
+                )
+
+            turn(0)
+            turn(1)
+            turn(2)
+            for b in range(blocks + 1):
+                if b + 3 < blocks:
+                    turn(b + 3)
+                if b < blocks:
+                    weigh(b)
+                if b >= 2 and b % 2 == 0:
+                    lay(b // 2 - 1)
+                if b < blocks:
+                    turn_back(b)
+            quantise(o, 0, TURNED, z[:])
+
+        acc = {}
+
+        def multiply(dh, c, o):
+            first = (dh, c) not in acc
+            if first:
+                acc[dh, c] = bank[(3, 5, 6, 7)[order.index(c)]] if dh == 0 else bank[(6, 7, 3, 5)[order.index(c)]]
+            nc.tensor.matmul_mx(
+                out=acc[dh, c][:],
+                lhsT=words[:, o, 2 * P * dh : 2 * P * (dh + 1)].bitcast(E2M1X4),
+                lhsT_scale=w_sc[:, o, P * dh : P * (dh + 1)],
+                rhs=codes[o][:, c * N : (c + 1) * N].bitcast(E5M2X4),
+                rhs_scale=scales[o][:, c * N : (c + 1) * N],
+                start=first,
+                stop=not first,
+            )
+
+        order = list(range(TURNED // N, CHUNKS)) + list(range(TURNED // N))
+        make_slope(slope_t[0])
+        g_d = keep.tile([P, PACK, DIRECT], F32, name="g_direct")
+        gather_direct(0, g_d, range(PACK))
+        g_t0 = gather_turned(0)
+        make_slope([slope_d[0][:, r, :] for r in range(PACK)])
+        nc.tensor.transpose(bank[4][:, :P], ew_rows[:], ident[:])
+        nc.scalar.copy(out=ew_t[:], in_=bank[4][:, : TURNED // P])
+        finish_direct(0, g_d)
+        finish_turned(0, g_t0)
+        for c in order[2:]:
+            multiply(0, c, 0)
+        make_slope(slope_t[1])
+        gather_direct(1, shared, (0, 1))
+        g_t1 = gather_turned(1)
+        gather_direct(1, shared, (2, 3))
+        make_slope([slope_d[1][:, r, :] for r in range(PACK)])
+        finish_direct(1, shared)
+        finish_turned(1, g_t1)
+
+        for c in order:
+            if c in order[:2]:
+                multiply(0, c, 0)
+            multiply(0, c, 1)
+            if c == order[-1]:
+                nc.vector.tensor_copy(out=dm[0][:, c * N : (c + 1) * N], in_=acc[0, c][:])
+            else:
+                nc.scalar.copy(out=dm[0][:, c * N : (c + 1) * N], in_=acc[0, c][:])
+        for c in order:
+            for o in reversed(range(PASSES)):
+                multiply(1, c, o)
+            nc.scalar.copy(out=dm[1][:, c * N : (c + 1) * N], in_=acc[1, c][:])
+
+        for dh in range(D // P):
+            cuts = [0, 1024, E] if dh == 0 else [0, 1024, 1792, E]
+            for a, b in zip(cuts, cuts[1:]):
+                picked = work.tile([P, b - a], F32, name="picked")
+                nc.vector.tensor_copy(picked[:], dm[dh][:].indirect(listed(src, a, b)))
+                res = work.tile([P, (b - a) // K], F32, name="res", bufs=5)
+                pairs = picked[:].rearrange("p (x j) -> p x j", j=K)
+                nc.vector.tensor_tensor(res[:], pairs[:, :, 0], pairs[:, :, 1], ADD)
+                nc.sync.dma_start(out=out[dh * P : (dh + 1) * P, a // K : b // K], in_=res[:])

@@ -46,6 +46,8 @@ def tile_attend_gmp_tnh_ew_kernel(tc, dyT, hE, ew, w_words, w_scales, offs, offs
         first_t = keep.tile([P, PACK, TURNED], F32, name="first_t")
         shared = keep.tile([P, PACK + 2, TURNED], F32, name="shared")
         slope_t = [[first_t[:, r, :] for r in range(PACK)], [shared[:, 2 + (r + 2) % PACK, :] for r in range(PACK)]]
+        staging = keep.tile([P, TURNED], F32, name="staging")
+        area = [keep.tile([P, PACK * TURNED], F32, name="area%d" % o, align_bytes=64) for o in range(PASSES)]
         bank = [psum.tile([P, N], F32, name="bank%d" % i) for i in range(8)]
         slope_d = [keep.tile([P, PACK, DIRECT], F32, name="slope_d%d" % o) for o in range(PASSES)]
         ew_d = keep.tile([P, DIRECT], F32, name="ew_d")
@@ -71,9 +73,9 @@ def tile_attend_gmp_tnh_ew_kernel(tc, dyT, hE, ew, w_words, w_scales, offs, offs
             nc.sync.dma_start(out=slope_t[0][r], in_=h_planes[0, r][:, :TURNED])
             if r == 0:
                 nc.sync.dma_start(out=ew_d[:, half:], in_=ew[:, TURNED + half :])
+                nc.sync.dma_start(out=ew_rows[: TURNED // P, :], in_=ew[0, :TURNED].rearrange("(b e) -> b e", e=P))
         for r in range(PACK):
             nc.sync.dma_start(out=slope_d[0][:, r, :], in_=h_planes[0, r][:, TURNED:])
-        nc.sync.dma_start(out=ew_rows[: TURNED // P, :], in_=ew[0, :TURNED].rearrange("(b e) -> b e", e=P))
         for r in range(PACK):
             nc.sync.dma_start(out=dy[1, r][:, :V], in_=dy_planes[1, r])
         for r in range(PACK):
@@ -91,12 +93,13 @@ def tile_attend_gmp_tnh_ew_kernel(tc, dyT, hE, ew, w_words, w_scales, offs, offs
         def listed(lst, a, b):
             return lst[:, a // 16 : b // 16]
 
-        def make_slope(s):
-            for r in range(PACK + 1):
-                if r < PACK:
-                    nc.scalar.activation(out=s[r], in_=s[r], func=ACT.Square)
+        def make_slope(s, last_square=None):
+            squares = s[:-1] + [s[-1] if last_square is None else last_square]
+            for r in range(len(s) + 1):
+                if r < len(s):
+                    nc.scalar.activation(out=squares[r], in_=s[r], func=ACT.Square)
                 if r > 0:
-                    nc.scalar.activation(out=s[r - 1], in_=s[r - 1], func=ACT.Copy, scale=-1.0, bias=1.0)
+                    nc.scalar.activation(out=s[r - 1], in_=squares[r - 1], func=ACT.Copy, scale=-1.0, bias=1.0)
 
         def gather_direct(o, g, planes):
             for r in planes:
@@ -105,7 +108,7 @@ def tile_attend_gmp_tnh_ew_kernel(tc, dyT, hE, ew, w_words, w_scales, offs, offs
                     nc.vector.tensor_tensor(g[:, r, a:b], dy[o, r][:].indirect(listed(dst, TURNED + a, TURNED + b)), ew_d[:, a:b], MULT)
 
         def gather_turned(o):
-            g = keep.tile([P, PACK, TURNED], F32, name="g_turned")
+            g = area[o][:].rearrange("p (t e) -> p t e", t=PACK)
             for r in range(PACK):
                 nc.vector.tensor_tensor(g[:, r, :], dy[o, r][:].indirect(listed(dst, 0, TURNED)), slope_t[o][r], MULT)
             return g
@@ -131,48 +134,51 @@ def tile_attend_gmp_tnh_ew_kernel(tc, dyT, hE, ew, w_words, w_scales, offs, offs
         def finish_turned(o, g):
             blocks = TURNED // P
             rows = {}
-            z = keep.tile([P, TURNED * PACK], BF16, name="dz_turned", align_bytes=64)
+            z = area[1 - o][:, : 2 * TURNED]
+            place = [4 * (b // 2 % 2) + 2 * (b // 4) + b % 2 for b in range(blocks)]
             there = [bank[b % 4][:].rearrange("e (t p) -> e t p", t=PACK) for b in range(blocks)]
             back = [bank[4 + pair % 2][:].rearrange("p (b u e) -> p b u e", b=2, u=2) for pair in range(blocks // 2)]
 
             def turn(b):
                 for t in range(PACK):
-                    nc.tensor.transpose(there[b][:, t, :], g[:, t, b * P : (b + 1) * P], ident[:])
+                    nc.tensor.transpose(there[b][:, t, :], g[:, t, place[b] * P : (place[b] + 1) * P], ident[:])
 
             def weigh(b):
-                zt = work.tile([P, PACK * P], BF16, name="dz_rows", bufs=4)
+                zt = staging[:, b % 4 * 2 * P : (b % 4 + 1) * 2 * P]
                 nc.scalar.activation(
-                    out=zt[:].rearrange("e (u p w) -> e u p w", u=2, w=2),
+                    out=zt.bitcast(BF16).rearrange("e (u p w) -> e u p w", u=2, w=2),
                     in_=there[b].rearrange("e (u w) p -> e u p w", w=2),
                     func=ACT.Copy,
-                    scale=ew_t[:, b : b + 1],
+                    scale=ew_t[:, place[b] : place[b] + 1],
                 )
                 rows[b] = zt
 
             def turn_back(b):
                 for u in range(2):
-                    nc.tensor.transpose(back[b // 2][:, b % 2, u, :], rows[b][:].bitcast(F32)[:, u * P : (u + 1) * P], ident[:])
+                    nc.tensor.transpose(back[b // 2][:, b % 2, u, :], rows[b][:, u * P : (u + 1) * P], ident[:])
 
             def lay(pair):
-                at = pair * N
+                at = place[2 * pair] * 2 * P
                 nc.scalar.copy(
-                    out=z[:].bitcast(F32)[:, at : at + N].rearrange("p (b e u) -> p b e u", b=2, u=2),
+                    out=z[:, at : at + N].rearrange("p (b e u) -> p b e u", b=2, u=2),
                     in_=back[pair].rearrange("p b u e -> p b e u"),
                 )
 
             turn(0)
             turn(1)
             turn(2)
-            for b in range(blocks + 1):
+            for b in range(blocks):
                 if b + 3 < blocks:
                     turn(b + 3)
                 if b < blocks:
                     weigh(b)
-                if b >= 2 and b % 2 == 0:
-                    lay(b // 2 - 1)
-                if b < blocks:
                     turn_back(b)
-            quantise(o, 0, TURNED, z[:])
+                if b >= 3 and b % 2 == 1:
+                    lay(b // 2 - 1)
+            lay(blocks // 2 - 1)
+            width = TURNED if o == 0 else N
+            for a in range(0, TURNED, width):
+                quantise(o, a, a + width, z[:, 2 * a : 2 * (a + width)].bitcast(BF16))
 
         acc = {}
 
@@ -192,12 +198,12 @@ def tile_attend_gmp_tnh_ew_kernel(tc, dyT, hE, ew, w_words, w_scales, offs, offs
 
         order = list(range(TURNED // N, CHUNKS)) + list(range(TURNED // N))
         make_slope(slope_t[0])
+        nc.tensor.transpose(bank[4][:, :P], ew_rows[:], ident[:])
+        nc.scalar.copy(out=ew_t[:], in_=bank[4][:, : TURNED // P])
         g_d = keep.tile([P, PACK, DIRECT], F32, name="g_direct")
         gather_direct(0, g_d, range(PACK))
         g_t0 = gather_turned(0)
-        make_slope([slope_d[0][:, r, :] for r in range(PACK)])
-        nc.tensor.transpose(bank[4][:, :P], ew_rows[:], ident[:])
-        nc.scalar.copy(out=ew_t[:], in_=bank[4][:, : TURNED // P])
+        make_slope([slope_d[0][:, r, :] for r in range(PACK)], staging[:])
         finish_direct(0, g_d)
         finish_turned(0, g_t0)
         for c in order[2:]:
@@ -206,7 +212,7 @@ def tile_attend_gmp_tnh_ew_kernel(tc, dyT, hE, ew, w_words, w_scales, offs, offs
         gather_direct(1, shared, (0, 1))
         g_t1 = gather_turned(1)
         gather_direct(1, shared, (2, 3))
-        make_slope([slope_d[1][:, r, :] for r in range(PACK)])
+        make_slope([slope_d[1][:, r, :] for r in range(PACK)], staging[:])
         finish_direct(1, shared)
         finish_turned(1, g_t1)
 
@@ -224,11 +230,12 @@ def tile_attend_gmp_tnh_ew_kernel(tc, dyT, hE, ew, w_words, w_scales, offs, offs
             nc.scalar.copy(out=dm[1][:, c * N : (c + 1) * N], in_=acc[1, c][:])
 
         for dh in range(D // P):
-            cuts = [0, 1024, E] if dh == 0 else [0, 1024, 1792, E]
+            cuts = [0, 1024, E] if dh == 0 else [0, 1024, 1536, E]
             for a, b in zip(cuts, cuts[1:]):
-                picked = work.tile([P, b - a], F32, name="picked")
+                picked = work.tile([P, b - a], F32, name="picked", bufs=3)
                 nc.vector.tensor_copy(picked[:], dm[dh][:].indirect(listed(src, a, b)))
                 res = work.tile([P, (b - a) // K], F32, name="res", bufs=5)
                 pairs = picked[:].rearrange("p (x j) -> p x j", j=K)
-                nc.vector.tensor_tensor(res[:], pairs[:, :, 0], pairs[:, :, 1], ADD)
+                adder = nc.vector if (dh, b) == (D // P - 1, E) else nc.gpsimd
+                adder.tensor_tensor(res[:], pairs[:, :, 0], pairs[:, :, 1], ADD)
                 nc.sync.dma_start(out=out[dh * P : (dh + 1) * P, a // K : b // K], in_=res[:])

from contextlib import ExitStack

import concourse.mybir as mybir
from concourse.masks import make_identity

V, K, E, D, DV = 1024, 2, 2048, 256, 1024
FLOPS = 2 * DV * D * E

F32 = mybir.dt.float32
BF16 = mybir.dt.bfloat16
I32 = mybir.dt.int32
U32 = mybir.dt.uint32
U16 = mybir.dt.uint16
U8 = mybir.dt.uint8
E5M2X4 = mybir.dt.float8_e5m2_x4
E2M1X4 = mybir.dt.float4_e2m1fn_x4
MULT = mybir.AluOpType.mult
ADD = mybir.AluOpType.add
ACT = mybir.ActivationFunctionType

P = 128
PACK = 4
PASSES = DV // (P * PACK)
N = 512
TURNED = 1024
DIRECT = E - TURNED
SPARE = 16
CHUNKS = E // N


def tile_attend_gmp_tnh_ew_kernel(tc, dyT, hE, ew, w_words, w_scales, offs, offs2, out):
    nc = tc.nc
    dy_planes = dyT.rearrange("(o p r) v -> o r p v", p=P, r=PACK)
    h_planes = hE.rearrange("(o p r) e -> o r p e", p=P, r=PACK)

    with ExitStack() as ctx:
        keep = ctx.enter_context(tc.tile_pool(name="keep", bufs=1))
        work = ctx.enter_context(tc.tile_pool(name="work", bufs=2))
        psum = ctx.enter_context(tc.psum_pool(name="psum", bufs=1))

        dst = keep.tile([P, E // 16], U16, name="dst")
        src = keep.tile([P, E // 16], U16, name="src")
        words = keep.tile([P, PASSES, 2 * D], U8, name="words", align_bytes=64)
        w_sc = keep.tile([P, PASSES, D], U8, name="w_sc", align_bytes=64)
        dy = {(o, r): keep.tile([P, V + SPARE], F32, name="dy%d%d" % (o, r)) for o in range(PASSES) for r in range(PACK)}
        first_t = keep.tile([P, PACK, TURNED], F32, name="first_t")
        shared = keep.tile([P, PACK + 2, TURNED], F32, name="shared")
        slope_t = [[first_t[:, r, :] for r in range(PACK)], [shared[:, 2 + (r + 2) % PACK, :] for r in range(PACK)]]
        staging = keep.tile([P, TURNED], F32, name="staging")
        area = [keep.tile([P, PACK * TURNED], F32, name="area%d" % o, align_bytes=64) for o in range(PASSES)]
        bank = [psum.tile([P, N], F32, name="bank%d" % i) for i in range(8)]
        slope_d = [keep.tile([P, PACK, DIRECT], F32, name="slope_d%d" % o) for o in range(PASSES)]
        ew_d = keep.tile([P, DIRECT], F32, name="ew_d")
        ew_rows = keep.tile([P, P], F32, name="ew_rows")
        ew_t = keep.tile([P, TURNED // P], F32, name="ew_t")
        ident = keep.tile([P, P], F32, name="ident")
        codes = [keep.tile([P, E], U32, name="codes%d" % o, align_bytes=64) for o in range(PASSES)]
        scales = [keep.tile([P, E], U8, name="scales%d" % o, align_bytes=64) for o in range(PASSES)]
        dm = [keep.tile([P, E], F32, name="dm%d" % dh) for dh in range(D // P)]

        for t in dy.values():
            nc.vector.memset(t[:, V:], 0.0)
        nc.vector.memset(w_sc[:].rearrange("p o d -> p (o d)").bitcast(U32), 0)
        nc.vector.memset(ew_rows[:], 0.0)
        make_identity(nc, ident[:])

        nc.sync.dma_start(dst[:], offs)
        half = DIRECT // 2
        for r in range(PACK):
            nc.sync.dma_start(out=dy[0, r][:, :V], in_=dy_planes[0, r])
            if r == 0:
                nc.sync.dma_start(out=ew_d[:, :half], in_=ew[:, TURNED : TURNED + half])
            nc.sync.dma_start(out=slope_t[0][r], in_=h_planes[0, r][:, :TURNED])
            if r == 0:
                nc.sync.dma_start(out=ew_d[:, half:], in_=ew[:, TURNED + half :])
                nc.sync.dma_start(out=ew_rows[: TURNED // P, :], in_=ew[0, :TURNED].rearrange("(b e) -> b e", e=P))
        for r in range(PACK):
            nc.sync.dma_start(out=slope_d[0][:, r, :], in_=h_planes[0, r][:, TURNED:])
        for r in range(PACK):
            nc.sync.dma_start(out=dy[1, r][:, :V], in_=dy_planes[1, r])
        for r in range(PACK):
            nc.sync.dma_start(out=slope_t[1][r], in_=h_planes[1, r][:, :TURNED])
        for r in range(PACK):
            nc.sync.dma_start(out=slope_d[1][:, r, :], in_=h_planes[1, r][:, TURNED:])
        nc.sync.dma_start(out=words[:].bitcast(I32), in_=w_words.rearrange("o p b -> p o b").bitcast(I32))
        for q in range(4):
            nc.sync.dma_start(
                out=w_sc[32 * q : 32 * q + 4, :, :].bitcast(I32),
                in_=w_scales[:, 4 * q : 4 * q + 4, :].rearrange("o f d -> f o d").bitcast(I32),
            )
        nc.sync.dma_start(src[:], offs2)

        def listed(lst, a, b):
            return lst[:, a // 16 : b // 16]

        def make_slope(s, last_square=None):
            squares = s[:-1] + [s[-1] if last_square is None else last_square]
            for r in range(len(s) + 1):
                if r < len(s):
                    nc.scalar.activation(out=squares[r], in_=s[r], func=ACT.Square)
                if r > 0:
                    nc.scalar.activation(out=s[r - 1], in_=squares[r - 1], func=ACT.Copy, scale=-1.0, bias=1.0)

        def gather_direct(o, g, planes):
            for r in planes:
                cuts = [0, half, DIRECT] if (o, r) == (0, 0) else [0, DIRECT]
                for a, b in zip(cuts, cuts[1:]):
                    nc.vector.tensor_tensor(g[:, r, a:b], dy[o, r][:].indirect(listed(dst, TURNED + a, TURNED + b)), ew_d[:, a:b], MULT)

        def gather_turned(o):
            g = area[o][:].rearrange("p (t e) -> p t e", t=PACK)
            for r in range(PACK):
                nc.vector.tensor_tensor(g[:, r, :], dy[o, r][:].indirect(listed(dst, 0, TURNED)), slope_t[o][r], MULT)
            return g

        def quantise(o, a, b, z):
            nc.vector.quantize_mx(out=codes[o][:, a:b].bitcast(E5M2X4), scales=scales[o][:, a:b], in_=z)

        def finish_direct(o, g):
            made = []
            for j in range(DIRECT // N):
                z = work.tile([P, N * PACK], BF16, name="dz_direct", align_bytes=64)
                cols = slice(j * N, (j + 1) * N)
                nc.vector.tensor_tensor(
                    z[:].rearrange("p (c i t) -> p c t i", i=2, t=PACK),
                    g[:, :PACK, cols].rearrange("p t (c i) -> p c t i", i=2),
                    slope_d[o][:, :, cols].rearrange("p t (c i) -> p c t i", i=2),
                    MULT,
                )
                made.append(z)
            for j, z in enumerate(made):
                quantise(o, TURNED + j * N, TURNED + (j + 1) * N, z[:])

        def finish_turned(o, g):
            blocks = TURNED // P
            rows = {}
            z = area[1 - o][:, : 2 * TURNED]
            place = [4 * (b // 2 % 2) + 2 * (b // 4) + b % 2 for b in range(blocks)]
            there = [bank[b % 4][:].rearrange("e (t p) -> e t p", t=PACK) for b in range(blocks)]
            back = [bank[4 + pair % 2][:].rearrange("p (b u e) -> p b u e", b=2, u=2) for pair in range(blocks // 2)]

            def turn(b):
                for t in range(PACK):
                    nc.tensor.transpose(there[b][:, t, :], g[:, t, place[b] * P : (place[b] + 1) * P], ident[:])

            def weigh(b):
                zt = staging[:, b % 4 * 2 * P : (b % 4 + 1) * 2 * P]
                nc.scalar.activation(
                    out=zt.bitcast(BF16).rearrange("e (u p w) -> e u p w", u=2, w=2),
                    in_=there[b].rearrange("e (u w) p -> e u p w", w=2),
                    func=ACT.Copy,
                    scale=ew_t[:, place[b] : place[b] + 1],
                )
                rows[b] = zt

            def turn_back(b):
                for u in range(2):
                    nc.tensor.transpose(back[b // 2][:, b % 2, u, :], rows[b][:, u * P : (u + 1) * P], ident[:])

            def lay(pair):
                at = place[2 * pair] * 2 * P
                nc.scalar.copy(
                    out=z[:, at : at + N].rearrange("p (b e u) -> p b e u", b=2, u=2),
                    in_=back[pair].rearrange("p b u e -> p b e u"),
                )

            turn(0)
            turn(1)
            turn(2)
            for b in range(blocks):
                if b + 3 < blocks:
                    turn(b + 3)
                if b < blocks:
                    weigh(b)
                    turn_back(b)
                if b >= 3 and b % 2 == 1:
                    lay(b // 2 - 1)
            lay(blocks // 2 - 1)
            width = TURNED if o == 0 else N
            for a in range(0, TURNED, width):
                quantise(o, a, a + width, z[:, 2 * a : 2 * (a + width)].bitcast(BF16))

        acc = {}

        def multiply(dh, c, o):
            first = (dh, c) not in acc
            if first:
                acc[dh, c] = bank[(3, 5, 6, 7)[order.index(c)]] if dh == 0 else bank[(6, 7, 3, 5)[order.index(c)]]
            nc.tensor.matmul_mx(
                out=acc[dh, c][:],
                lhsT=words[:, o, 2 * P * dh : 2 * P * (dh + 1)].bitcast(E2M1X4),
                lhsT_scale=w_sc[:, o, P * dh : P * (dh + 1)],
                rhs=codes[o][:, c * N : (c + 1) * N].bitcast(E5M2X4),
                rhs_scale=scales[o][:, c * N : (c + 1) * N],
                start=first,
                stop=not first,
            )

        order = list(range(TURNED // N, CHUNKS)) + list(range(TURNED // N))
        make_slope(slope_t[0])
        nc.tensor.transpose(bank[4][:, :P], ew_rows[:], ident[:])
        nc.scalar.copy(out=ew_t[:], in_=bank[4][:, : TURNED // P])
        g_d = keep.tile([P, PACK, DIRECT], F32, name="g_direct")
        gather_direct(0, g_d, range(PACK))
        g_t0 = gather_turned(0)
        make_slope([slope_d[0][:, r, :] for r in range(PACK)], staging[:])
        finish_direct(0, g_d)
        finish_turned(0, g_t0)
        for c in order[2:]:
            multiply(0, c, 0)
        make_slope(slope_t[1])
        gather_direct(1, shared, (0, 1))
        g_t1 = gather_turned(1)
        gather_direct(1, shared, (2, 3))
        make_slope([slope_d[1][:, r, :] for r in range(PACK)], staging[:])
        finish_direct(1, shared)
        finish_turned(1, g_t1)

        for c in order:
            if c in order[:2]:
                multiply(0, c, 0)
            multiply(0, c, 1)
            if c == order[-1]:
                nc.vector.tensor_copy(out=dm[0][:, c * N : (c + 1) * N], in_=acc[0, c][:])
            else:
                nc.scalar.copy(out=dm[0][:, c * N : (c + 1) * N], in_=acc[0, c][:])
        for c in order:
            for o in reversed(range(PASSES)):
                multiply(1, c, o)
            nc.scalar.copy(out=dm[1][:, c * N : (c + 1) * N], in_=acc[1, c][:])

        for dh in range(D // P):
            cuts = [0, 1024, E] if dh == 0 else [0, 1024, 1536, E]
            for a, b in zip(cuts, cuts[1:]):
                picked = work.tile([P, b - a], F32, name="picked", bufs=3)
                nc.vector.tensor_copy(picked[:], dm[dh][:].indirect(listed(src, a, b)))
                res = work.tile([P, (b - a) // K], F32, name="res", bufs=5)
                pairs = picked[:].rearrange("p (x j) -> p x j", j=K)
                adder = nc.vector if (dh, b) == (D // P - 1, E) else nc.gpsimd
                adder.tensor_tensor(res[:], pairs[:, :, 0], pairs[:, :, 1], ADD)
                nc.sync.dma_start(out=out[dh * P : (dh + 1) * P, a // K : b // K], in_=res[:])
